import numpy as np
import ml_dtypes

BF16 = ml_dtypes.bfloat16


def bf(x):
    return np.asarray(x, np.float32).astype(BF16)


def f32(x):
    return np.asarray(x, np.float32)


def f64(x):
    return np.asarray(x).astype(np.float64)


def striped(idx):
    return np.tile(idx.reshape(-1, 16).T, (8, 1))


def rows(idx, k):
    return np.tile(idx, (k, 1))


def look(tab, idx):
    return np.take_along_axis(f64(tab), rows(idx, len(tab)), axis=1)


K, S, D, V, N, M = 512, 2048, 2, 512, 1024, 128


def setup_inputs():
    return {"tab": f32(np.random.standard_normal((K, S))), "ctr": f32(1.0 * np.random.standard_normal((K, V))), "w": bf(np.random.standard_normal((K, M)) / np.sqrt(K)), "b": f32(0.5 * np.random.standard_normal((M, 1))), "offs": striped(np.random.permutation(S)[:N])}


def reference(tab, ctr, w, b, offs):
    idx = offs[:16].T.reshape(-1)
    e = [np.abs(look(tab, idx[d * V:(d + 1) * V]) - f64(ctr)) for d in range(D)]
    x = sum(np.minimum(v, 1.0) * (v - 0.5 * np.minimum(v, 1.0)) for v in e)
    return np.maximum(f64(w).T @ x + f64(b), 0.0)

@@ -1,0 +1,83 @@
+import math
+
+import concourse.mybir as mybir
+
+F32, BF16, U16 = mybir.dt.float32, mybir.dt.bfloat16, mybir.dt.uint16
+ALU = mybir.AluOpType
+ACT = mybir.ActivationFunctionType
+
+P = 128
+LIST_ROWS = 16
+PIECE = 256
+
+FLOPS = 2 * 512 * 128 * 512
+
+
+def tile_lookup_huber_relu_kernel(tc, tab, ctr, w, b, offs, out):
+    nc = tc.nc
+    rows, table_cols = tab.shape
+    out_rows, out_cols = out.shape
+    blocks = rows // P
+    lookups = offs.shape[1] * LIST_ROWS // out_cols
+    pieces = out_cols // PIECE
+
+    tab_blocks = tab.rearrange("(p k) s -> k p s", k=blocks)
+    ctr_blocks = ctr.rearrange("(p k) j -> k p j", k=blocks)
+    w_rows = w.rearrange("(p k) m -> p (k m)", k=blocks)
+
+    with (
+        tc.tile_pool(name="held", bufs=1) as held,
+        tc.tile_pool(name="work", bufs=3) as work,
+        tc.psum_pool(name="psum", bufs=1) as psum,
+    ):
+        offsets = held.tile([P, offs.shape[1]], U16, name="offsets")
+        windows = [held.tile([P, table_cols], F32, name=f"window{k}") for k in range(blocks)]
+        targets = [held.tile([P, out_cols], F32, name=f"target{k}") for k in range(blocks)]
+        w_bf16 = held.tile([P, blocks * out_rows], BF16, name="w_bf16")
+        w_f32 = held.tile([P, blocks * out_rows], F32, name="w_f32")
+        bias = held.tile([P, 1], F32, name="bias")
+        sums = [psum.tile([P, PIECE], F32, name=f"sum{i}") for i in range(pieces)]
+
+        nc.sync.dma_start(offsets[:], offs)
+        for k in range(blocks):
+            nc.sync.dma_start(windows[k][:], tab_blocks[k])
+            nc.sync.dma_start(targets[k][:], ctr_blocks[k])
+            if k == 0:
+                nc.sync.dma_start(w_bf16[:], w_rows)
+        nc.sync.dma_start(bias[:], b)
+        nc.scalar.activation(w_f32[:], w_bf16[:], ACT.Copy)
+
+        for k in range(blocks):
+            for i in range(pieces):
+                first = i * PIECE
+                diff = work.tile([P, lookups * PIECE], F32, name="diff")
+                for d in range(lookups):
+                    entry = d * out_cols + first
+                    picks = offsets[:, entry // LIST_ROWS : (entry + PIECE) // LIST_ROWS]
+                    nc.vector.tensor_tensor(
+                        diff[:, d * PIECE : (d + 1) * PIECE],
+                        windows[k][:].indirect(picks),
+                        targets[k][:, first : first + PIECE],
+                        ALU.subtract,
+                    )
+                dist = work.tile([P, lookups * PIECE], F32, name="dist")
+                half_square = work.tile([P, lookups * PIECE], F32, name="half_square")
+                excess = work.tile([P, lookups * PIECE], F32, name="excess")
+                loss = work.tile([P, lookups * PIECE], F32, name="loss")
+                nc.scalar.activation(dist[:], diff[:], ACT.Abs)
+                nc.scalar.activation(half_square[:], diff[:], ACT.Square, scale=math.sqrt(0.5))
+                nc.scalar.activation(excess[:], dist[:], ACT.Relu, bias=-1.0)
+                nc.vector.scalar_tensor_tensor(loss[:], half_square[:], 0.5, excess[:], ALU.min, ALU.add)
+                for d in range(lookups):
+                    nc.tensor.matmul(
+                        sums[i][:],
+                        w_f32[:, k * out_rows : (k + 1) * out_rows],
+                        loss[:, d * PIECE : (d + 1) * PIECE],
+                        start=(k == 0 and d == 0),
+                        stop=(k == blocks - 1 and d == lookups - 1),
+                    )
+
+        for i in range(pieces):
+            result = work.tile([P, PIECE], F32, name="result")
+            nc.scalar.activation(result[:], sums[i][:], ACT.Relu, bias=bias[:])
+            nc.sync.dma_start(out[:, i * PIECE : (i + 1) * PIECE], result[:])

@@ -8,7 +8,8 @@ ACT = mybir.ActivationFunctionType
 
 P = 128
 LIST_ROWS = 16
-PIECE = 256
+WIDE = 256
+NARROW = 128
 
 FLOPS = 2 * 512 * 128 * 512
 
@@ -19,7 +20,12 @@ def tile_lookup_huber_relu_kernel(tc, tab, ctr, w, b, offs, out):
     out_rows, out_cols = out.shape
     blocks = rows // P
     lookups = offs.shape[1] * LIST_ROWS // out_cols
-    pieces = out_cols // PIECE
+
+    wide_steps = [(k, first) for k in range(blocks) for first in range(0, out_cols, WIDE)]
+    steps = []
+    for k, first in wide_steps:
+        width = NARROW if (k, first) in (wide_steps[0], wide_steps[-1]) else WIDE
+        steps.extend((k, col, width) for col in range(first, first + WIDE, width))
 
     tab_blocks = tab.rearrange("(p k) s -> k p s", k=blocks)
     ctr_blocks = ctr.rearrange("(p k) j -> k p j", k=blocks)
@@ -27,7 +33,8 @@ def tile_lookup_huber_relu_kernel(tc, tab, ctr, w, b, offs, out):
 
     with (
         tc.tile_pool(name="held", bufs=1) as held,
-        tc.tile_pool(name="work", bufs=3) as work,
+        tc.tile_pool(name="diffs", bufs=3) as diffs,
+        tc.tile_pool(name="work", bufs=4) as work,
         tc.psum_pool(name="psum", bufs=1) as psum,
     ):
         offsets = held.tile([P, offs.shape[1]], U16, name="offsets")
@@ -36,48 +43,50 @@ def tile_lookup_huber_relu_kernel(tc, tab, ctr, w, b, offs, out):
         w_bf16 = held.tile([P, blocks * out_rows], BF16, name="w_bf16")
         w_f32 = held.tile([P, blocks * out_rows], F32, name="w_f32")
         bias = held.tile([P, 1], F32, name="bias")
-        sums = [psum.tile([P, PIECE], F32, name=f"sum{i}") for i in range(pieces)]
+        result = held.tile([P, out_cols], F32, name="result")
+        sums = [psum.tile([P, NARROW], F32, name=f"sum{i}") for i in range(out_cols // NARROW)]
 
         nc.sync.dma_start(offsets[:], offs)
-        for k in range(blocks):
+        nc.sync.dma_start(w_bf16[:], w_rows)
+        nc.sync.dma_start(windows[0][:], tab_blocks[0])
+        nc.sync.dma_start(targets[0][:, :WIDE], ctr_blocks[0][:, :WIDE])
+        nc.sync.dma_start(targets[0][:, WIDE:], ctr_blocks[0][:, WIDE:])
+        for k in range(1, blocks):
             nc.sync.dma_start(windows[k][:], tab_blocks[k])
             nc.sync.dma_start(targets[k][:], ctr_blocks[k])
-            if k == 0:
-                nc.sync.dma_start(w_bf16[:], w_rows)
         nc.sync.dma_start(bias[:], b)
-        nc.scalar.activation(w_f32[:], w_bf16[:], ACT.Copy)
+        nc.vector.tensor_copy(w_f32[:], w_bf16[:])
 
-        for k in range(blocks):
-            for i in range(pieces):
-                first = i * PIECE
-                diff = work.tile([P, lookups * PIECE], F32, name="diff")
-                for d in range(lookups):
-                    entry = d * out_cols + first
-                    picks = offsets[:, entry // LIST_ROWS : (entry + PIECE) // LIST_ROWS]
-                    nc.vector.tensor_tensor(
-                        diff[:, d * PIECE : (d + 1) * PIECE],
-                        windows[k][:].indirect(picks),
-                        targets[k][:, first : first + PIECE],
-                        ALU.subtract,
-                    )
-                dist = work.tile([P, lookups * PIECE], F32, name="dist")
-                half_square = work.tile([P, lookups * PIECE], F32, name="half_square")
-                excess = work.tile([P, lookups * PIECE], F32, name="excess")
-                loss = work.tile([P, lookups * PIECE], F32, name="loss")
-                nc.scalar.activation(dist[:], diff[:], ACT.Abs)
-                nc.scalar.activation(half_square[:], diff[:], ACT.Square, scale=math.sqrt(0.5))
-                nc.scalar.activation(excess[:], dist[:], ACT.Relu, bias=-1.0)
-                nc.vector.scalar_tensor_tensor(loss[:], half_square[:], 0.5, excess[:], ALU.min, ALU.add)
+        for k, first, width in steps:
+            diff = diffs.tile([P, lookups * width], F32, name="diff")
+            for d in range(lookups):
+                entry = d * out_cols + first
+                picks = offsets[:, entry // LIST_ROWS : (entry + width) // LIST_ROWS]
+                nc.vector.tensor_tensor(
+                    diff[:, d * width : (d + 1) * width],
+                    windows[k][:].indirect(picks),
+                    targets[k][:, first : first + width],
+                    ALU.subtract,
+                )
+            dist = work.tile([P, lookups * width], F32, name="dist")
+            half_square = work.tile([P, lookups * width], F32, name="half_square")
+            excess = work.tile([P, lookups * width], F32, name="excess")
+            loss = work.tile([P, lookups * width], F32, name="loss")
+            nc.scalar.activation(dist[:], diff[:], ACT.Abs)
+            nc.scalar.activation(half_square[:], diff[:], ACT.Square, scale=math.sqrt(0.5))
+            nc.scalar.activation(excess[:], dist[:], ACT.Relu, bias=-1.0)
+            nc.vector.scalar_tensor_tensor(loss[:], half_square[:], 0.5, excess[:], ALU.min, ALU.add)
+            for col in range(0, width, NARROW):
                 for d in range(lookups):
                     nc.tensor.matmul(
-                        sums[i][:],
+                        sums[(first + col) // NARROW][:],
                         w_f32[:, k * out_rows : (k + 1) * out_rows],
-                        loss[:, d * PIECE : (d + 1) * PIECE],
+                        loss[:, d * width + col : d * width + col + NARROW],
                         start=(k == 0 and d == 0),
                         stop=(k == blocks - 1 and d == lookups - 1),
                     )
 
-        for i in range(pieces):
-            result = work.tile([P, PIECE], F32, name="result")
-            nc.scalar.activation(result[:], sums[i][:], ACT.Relu, bias=bias[:])
-            nc.sync.dma_start(out[:, i * PIECE : (i + 1) * PIECE], result[:])
+        for i, total in enumerate(sums):
+            cols = slice(i * NARROW, (i + 1) * NARROW)
+            nc.scalar.activation(result[:, cols], total[:], ACT.Relu, bias=bias[:])
+            nc.sync.dma_start(out[:, cols], result[:, cols])

@@ -24,7 +24,7 @@ def tile_lookup_huber_relu_kernel(tc, tab, ctr, w, b, offs, out):
     wide_steps = [(k, first) for k in range(blocks) for first in range(0, out_cols, WIDE)]
     steps = []
     for k, first in wide_steps:
-        width = NARROW if (k, first) in (wide_steps[0], wide_steps[-1]) else WIDE
+        width = NARROW if (k, first) == wide_steps[0] or k == blocks - 1 else WIDE
         steps.extend((k, col, width) for col in range(first, first + WIDE, width))
 
     tab_blocks = tab.rearrange("(p k) s -> k p s", k=blocks)
@@ -46,9 +46,9 @@ def tile_lookup_huber_relu_kernel(tc, tab, ctr, w, b, offs, out):
         result = held.tile([P, out_cols], F32, name="result")
         sums = [psum.tile([P, NARROW], F32, name=f"sum{i}") for i in range(out_cols // NARROW)]
 
-        nc.sync.dma_start(offsets[:], offs)
         nc.sync.dma_start(w_bf16[:], w_rows)
         nc.sync.dma_start(windows[0][:], tab_blocks[0])
+        nc.sync.dma_start(offsets[:], offs)
         nc.sync.dma_start(targets[0][:, :WIDE], ctr_blocks[0][:, :WIDE])
         nc.sync.dma_start(targets[0][:, WIDE:], ctr_blocks[0][:, WIDE:])
         for k in range(1, blocks):

import math

import concourse.mybir as mybir

F32, BF16, U16 = mybir.dt.float32, mybir.dt.bfloat16, mybir.dt.uint16
ALU = mybir.AluOpType
ACT = mybir.ActivationFunctionType

P = 128
LIST_ROWS = 16
WIDE = 256
NARROW = 128

FLOPS = 2 * 512 * 128 * 512


def tile_lookup_huber_relu_kernel(tc, tab, ctr, w, b, offs, out):
    nc = tc.nc
    rows, table_cols = tab.shape
    out_rows, out_cols = out.shape
    blocks = rows // P
    lookups = offs.shape[1] * LIST_ROWS // out_cols

    wide_steps = [(k, first) for k in range(blocks) for first in range(0, out_cols, WIDE)]
    steps = []
    for k, first in wide_steps:
        width = NARROW if (k, first) == wide_steps[0] or k == blocks - 1 else WIDE
        steps.extend((k, col, width) for col in range(first, first + WIDE, width))

    tab_blocks = tab.rearrange("(p k) s -> k p s", k=blocks)
    ctr_blocks = ctr.rearrange("(p k) j -> k p j", k=blocks)
    w_rows = w.rearrange("(p k) m -> p (k m)", k=blocks)

    with (
        tc.tile_pool(name="held", bufs=1) as held,
        tc.tile_pool(name="diffs", bufs=3) as diffs,
        tc.tile_pool(name="work", bufs=4) as work,
        tc.psum_pool(name="psum", bufs=1) as psum,
    ):
        offsets = held.tile([P, offs.shape[1]], U16, name="offsets")
        windows = [held.tile([P, table_cols], F32, name=f"window{k}") for k in range(blocks)]
        targets = [held.tile([P, out_cols], F32, name=f"target{k}") for k in range(blocks)]
        w_bf16 = held.tile([P, blocks * out_rows], BF16, name="w_bf16")
        w_f32 = held.tile([P, blocks * out_rows], F32, name="w_f32")
        bias = held.tile([P, 1], F32, name="bias")
        result = held.tile([P, out_cols], F32, name="result")
        sums = [psum.tile([P, NARROW], F32, name=f"sum{i}") for i in range(out_cols // NARROW)]

        nc.sync.dma_start(w_bf16[:], w_rows)
        nc.sync.dma_start(windows[0][:], tab_blocks[0])
        nc.sync.dma_start(offsets[:], offs)
        nc.sync.dma_start(targets[0][:, :WIDE], ctr_blocks[0][:, :WIDE])
        nc.sync.dma_start(targets[0][:, WIDE:], ctr_blocks[0][:, WIDE:])
        for k in range(1, blocks):
            nc.sync.dma_start(windows[k][:], tab_blocks[k])
            nc.sync.dma_start(targets[k][:], ctr_blocks[k])
        nc.sync.dma_start(bias[:], b)
        nc.vector.tensor_copy(w_f32[:], w_bf16[:])

        for k, first, width in steps:
            diff = diffs.tile([P, lookups * width], F32, name="diff")
            for d in range(lookups):
                entry = d * out_cols + first
                picks = offsets[:, entry // LIST_ROWS : (entry + width) // LIST_ROWS]
                nc.vector.tensor_tensor(
                    diff[:, d * width : (d + 1) * width],
                    windows[k][:].indirect(picks),
                    targets[k][:, first : first + width],
                    ALU.subtract,
                )
            dist = work.tile([P, lookups * width], F32, name="dist")
            half_square = work.tile([P, lookups * width], F32, name="half_square")
            excess = work.tile([P, lookups * width], F32, name="excess")
            loss = work.tile([P, lookups * width], F32, name="loss")
            nc.scalar.activation(dist[:], diff[:], ACT.Abs)
            nc.scalar.activation(half_square[:], diff[:], ACT.Square, scale=math.sqrt(0.5))
            nc.scalar.activation(excess[:], dist[:], ACT.Relu, bias=-1.0)
            nc.vector.scalar_tensor_tensor(loss[:], half_square[:], 0.5, excess[:], ALU.min, ALU.add)
            for col in range(0, width, NARROW):
                for d in range(lookups):
                    nc.tensor.matmul(
                        sums[(first + col) // NARROW][:],
                        w_f32[:, k * out_rows : (k + 1) * out_rows],
                        loss[:, d * width + col : d * width + col + NARROW],
                        start=(k == 0 and d == 0),
                        stop=(k == blocks - 1 and d == lookups - 1),
                    )

        for i, total in enumerate(sums):
            cols = slice(i * NARROW, (i + 1) * NARROW)
            nc.scalar.activation(result[:, cols], total[:], ACT.Relu, bias=bias[:])
            nc.sync.dma_start(out[:, cols], result[:, cols])
